import numpy as np
import ml_dtypes


def mxq(x, axis, fmt="e4m3"):
    dtype, down = {"e4m3": (ml_dtypes.float8_e4m3fn, 7), "e5m2": (ml_dtypes.float8_e5m2, 14)}[fmt]
    v = np.moveaxis(np.asarray(x, np.float32).astype(ml_dtypes.bfloat16).astype(np.float64), axis, -1)
    blocks = v.reshape(v.shape[:-1] + (-1, 32))
    amax = np.abs(blocks).max(-1, keepdims=True)
    byte = np.maximum(np.where(amax > 0, np.frexp(amax)[1] - 1 + 127, 0) - down, 1)
    scale = np.exp2(byte - 127.0)
    codes = (blocks / scale).astype(np.float32).astype(dtype).astype(np.float64)
    return np.moveaxis((codes * scale).reshape(v.shape), -1, axis)


WIDE = False


def mx_kscale(k):
    if not WIDE:
        return np.ones(k)
    levels = np.array([10, -10, 5, -5, 0])
    if k % 512:
        return np.exp2(np.random.permutation(np.resize(levels, k // 32))).repeat(32)
    a = np.empty((k // 512, 16))
    for p in range(k // 512):
        a[p, :8] = np.random.permutation(np.resize(levels, 8))
        for g in range(8):
            far = levels[np.abs(levels - a[p, g]) >= 10]
            a[p, g + 8] = far[np.random.randint(len(far))]
    return np.exp2(a.ravel()).repeat(32)


def f64(x):
    return np.asarray(x).astype(np.float64)


def striped(idx):
    return np.tile(idx.reshape(-1, 16).T, (8, 1)).astype(np.uint16)


def unstriped(offs):
    return offs[:16].T.reshape(-1).astype(np.int64)


def pack_weight(w):
    k, n = w.shape
    w = f64(np.asarray(w, np.float32).astype(ml_dtypes.bfloat16)).reshape(k // 32, 32, n)
    amax = np.abs(w).max(1)
    byte = np.clip(np.where(amax > 0, np.frexp(amax)[1] - 1 + 127 - 7, 1), 1, 254)
    scaled = (w * np.exp2(127.0 - byte)[:, None, :]).reshape(k, n).astype(np.float32)
    words = np.ascontiguousarray(scaled.reshape(k // 512, 128, 4, n).transpose(0, 1, 3, 2)).astype(ml_dtypes.float8_e4m3fn).view(np.uint8)
    return words, np.ascontiguousarray(byte.astype(np.uint8).reshape(k // 512, 16, n))


def unpack_weight(words, scales):
    g, p, n, _ = words.shape
    vals = np.ascontiguousarray(words).view(ml_dtypes.float8_e4m3fn).astype(np.float64) * np.repeat(np.exp2(scales.astype(np.float64) - 127.0), 8, axis=1)[..., None]
    return vals.transpose(0, 1, 3, 2).reshape(g * 512, n)


K, T, S, N = 1024, 1024, 512, 128


def setup_inputs():
    n = np.random.standard_normal
    s = mx_kscale(K)[:, None]
    packed_xT = pack_weight(n((K, T)) * s)
    packed_w1 = pack_weight(n((K, N)) / np.sqrt(2 * K) / s)
    packed_w2 = pack_weight(n((K, N)) / np.sqrt(2 * K) / s)
    packed_w3 = pack_weight(n((K, N)) / np.sqrt(2 * K) / s)
    packed_w4 = pack_weight(n((K, N)) / np.sqrt(2 * K) / s)
    return {
        "x_words": packed_xT[0],
        "x_scales": packed_xT[1],
        "eT": (n((K, S)) * s).astype(np.float32),
        "w1_words": packed_w1[0],
        "w1_scales": packed_w1[1],
        "w2_words": packed_w2[0],
        "w2_scales": packed_w2[1],
        "w3_words": packed_w3[0],
        "w3_scales": packed_w3[1],
        "w4_words": packed_w4[0],
        "w4_scales": packed_w4[1],
        "dec": (n((N, S))).astype(np.float32),
        "offs": striped(np.random.permutation(T)[:S]),
    }


def reference(x_words, x_scales, eT, w1_words, w1_scales, w2_words, w2_scales, w3_words, w3_scales, w4_words, w4_scales, dec, offs):
    eTq = mxq(f64(eT), 0, "e4m3")
    xq = unpack_weight(x_words, x_scales)[:, unstriped(offs)]
    g = unpack_weight(w1_words, w1_scales).T @ eTq + unpack_weight(w2_words, w2_scales).T @ xq
    h = unpack_weight(w3_words, w3_scales).T @ eTq + unpack_weight(w4_words, w4_scales).T @ xq
    return f64(dec) * g + h + f64(dec)

@@ -1,0 +1,118 @@
+from contextlib import ExitStack
+
+import concourse.mybir as mybir
+
+K, T, S, N = 1024, 1024, 512, 128
+P = 128
+PACK = 4
+K_PASS = P * PACK
+PASSES = K // K_PASS
+FLOPS = 2 * 4 * K * N * S
+
+F32 = mybir.dt.float32
+BF16 = mybir.dt.bfloat16
+I32 = mybir.dt.int32
+U32 = mybir.dt.uint32
+U16 = mybir.dt.uint16
+U8 = mybir.dt.uint8
+FP8X4 = mybir.dt.float8_e4m3fn_x4
+ADD = mybir.AluOpType.add
+MULT = mybir.AluOpType.mult
+
+PIECES = [(0, 0, 256, 128), (1, 0, 256, 128), (0, 256, 256, 128), (1, 256, 256, 96)]
+BLOCKS = [(0, 256), (256, 256)]
+
+
+def tile_picked_zcft_add_p_kernel(
+    tc, x_words, x_scales, eT, w1_words, w1_scales, w2_words, w2_scales,
+    w3_words, w3_scales, w4_words, w4_scales, dec, offs, out
+):
+    nc = tc.nc
+    w_words = [w1_words, w2_words, w3_words, w4_words]
+    w_scales = [w1_scales, w2_scales, w3_scales, w4_scales]
+    with ExitStack() as ctx:
+        keep = ctx.enter_context(tc.tile_pool(name="keep", bufs=1))
+        psum = ctx.enter_context(tc.psum_pool(name="psum", bufs=1))
+
+        offsets = keep.tile([P, S // 16], U16, name="offsets")
+        x_scale_table = keep.tile([P, T], U8, name="x_scale_table", align_bytes=64)
+        w_scale = keep.tile([P, 4, PASSES, N], U8, name="w_scale", align_bytes=64)
+        w_stage = keep.tile([16, 4, PASSES, N], U8, name="w_stage", tag="stage_then_dec", align_bytes=64)
+        nc.gpsimd.memset(x_scale_table[:].bitcast(I32), 0)
+        nc.vector.memset(w_scale[:].bitcast(I32), 0)
+
+        x_table = [keep.tile([P, T], I32, name="x_table%d" % o, align_bytes=64) for o in range(PASSES)]
+        w_code = [keep.tile([P, PASSES, N], I32, name="w_code%d" % i, align_bytes=64) for i in range(4)]
+        e_raw = [keep.tile([P, PACK, w], F32, name="e_raw%d" % i, align_bytes=64) for i, (o, c, w, s) in enumerate(PIECES)]
+
+        def load_x(o):
+            nc.sync.dma_start(out=x_table[o][:], in_=x_words[o].rearrange("p c r -> p (c r)").bitcast(I32))
+
+        def load_w(i):
+            nc.sync.dma_start(out=w_code[i][:], in_=w_words[i].rearrange("o p c r -> p o (c r)").bitcast(I32))
+
+        def load_e(i):
+            o, c, w, s = PIECES[i]
+            rows = eT[o * K_PASS:(o + 1) * K_PASS, c:c + w]
+            nc.sync.dma_start(out=e_raw[i][:], in_=rows.rearrange("(p j) w -> p j w", j=PACK))
+
+        nc.sync.dma_start(offsets[:], offs)
+        load_x(0)
+        for i in range(4):
+            nc.scalar.dma_start(out=w_stage[:, i].bitcast(I32), in_=w_scales[i].rearrange("o r c -> r o c").bitcast(I32))
+        load_x(1)
+        for q in range(4):
+            nc.gpsimd.dma_start(out=x_scale_table[32 * q:32 * q + 8, :].bitcast(I32), in_=x_scales[:, 4 * q:4 * q + 4, :].bitcast(I32))
+        warm = keep.tile([P, 2], F32, name="warm")
+        nc.vector.memset(warm[:, 0:1], 0.0)
+        nc.scalar.copy(out=warm[:, 1:2], in_=warm[:, 0:1])
+        for i in (1, 3, 0, 2):
+            load_w(i)
+        for i in range(len(PIECES)):
+            load_e(i)
+        for q in range(4):
+            nc.scalar.dma_start(out=w_scale[32 * q:32 * q + 4].bitcast(I32), in_=w_stage[4 * q:4 * q + 4].bitcast(I32))
+        dec_sb = keep.tile([P, S], F32, name="dec_sb", tag="stage_then_dec", align_bytes=64)
+        nc.sync.dma_start(out=dec_sb[:], in_=dec)
+
+        x_code = [keep.tile([P, S], U32, name="x_code%d" % o, align_bytes=64) for o in range(PASSES)]
+        x_scale = keep.tile([P, S], U8, name="x_scale", align_bytes=64)
+        nc.vector.tensor_copy(x_code[0][:], x_table[0][:].bitcast(U32).indirect(offsets[:]))
+        nc.vector.tensor_copy(x_scale[:], x_scale_table[:].indirect(offsets[:]))
+        nc.vector.tensor_copy(x_code[1][:], x_table[1][:].bitcast(U32).indirect(offsets[:]))
+
+        acc = [[psum.tile([P, w], F32, name="acc%d_%d" % (b, h)) for h in range(2)] for b, (c, w) in enumerate(BLOCKS)]
+
+        def product(b, h, i, o, codes, scales, start, stop):
+            nc.tensor.matmul_mx(
+                out=acc[b][h][:], lhsT=w_code[i][:, o, :].bitcast(FP8X4), lhsT_scale=w_scale[:, i, o, :],
+                rhs=codes.bitcast(FP8X4), rhs_scale=scales, start=start, stop=stop)
+
+        for o in range(PASSES):
+            for b, (c, w) in enumerate(BLOCKS):
+                for h in range(2):
+                    product(b, h, 2 * h + 1, o, x_code[o][:, c:c + w], x_scale[4 * o:, c:c + w], o == 0, False)
+
+        def interleave(copy, dst, src):
+            copy(out=dst.rearrange("p (c i) t -> p c t i", i=4), in_=src.rearrange("p t (c i) -> p c t i", i=4))
+
+        for i, (o, c, w, s) in enumerate(PIECES):
+            grouped = keep.tile([P, w, PACK], BF16, name="grouped%d" % i, align_bytes=64)
+            if s > 0:
+                interleave(nc.scalar.copy, grouped[:, :s, :], e_raw[i][:, :, :s])
+            if s < w:
+                interleave(nc.vector.tensor_copy, grouped[:, s:, :], e_raw[i][:, :, s:])
+            e_code = keep.tile([P, w], U32, name="e_code%d" % i, align_bytes=64)
+            e_scale = keep.tile([P, w], U8, name="e_scale%d" % i, align_bytes=64)
+            nc.vector.quantize_mx(out=e_code[:].bitcast(FP8X4), scales=e_scale[:], in_=grouped[:].rearrange("p w j -> p (w j)"))
+            for b, (bc, bw) in enumerate(BLOCKS):
+                if c <= bc < c + w:
+                    cols = slice(bc - c, bc - c + bw)
+                    for h in range(2):
+                        product(b, h, 2 * h, o, e_code[:, cols], e_scale[:, cols], False, o == PASSES - 1)
+                    if o == PASSES - 1:
+                        scaled = keep.tile([P, bw], F32, name="scaled%d" % b, align_bytes=64)
+                        result = keep.tile([P, bw], F32, name="result%d" % b, align_bytes=64)
+                        nc.vector.scalar_tensor_tensor(scaled[:], acc[b][0][:], 1.0, dec_sb[:, bc:bc + bw], ADD, MULT)
+                        nc.vector.tensor_tensor(result[:], acc[b][1][:], scaled[:], ADD)
+                        nc.sync.dma_start(out=out[:, bc:bc + bw], in_=result[:])

@@ -32,18 +32,23 @@ def tile_picked_zcft_add_p_kernel(
     w_scales = [w1_scales, w2_scales, w3_scales, w4_scales]
     with ExitStack() as ctx:
         keep = ctx.enter_context(tc.tile_pool(name="keep", bufs=1))
+        shared = ctx.enter_context(tc.tile_pool(name="shared", bufs=1))
         psum = ctx.enter_context(tc.psum_pool(name="psum", bufs=1))
 
         offsets = keep.tile([P, S // 16], U16, name="offsets")
         x_scale_table = keep.tile([P, T], U8, name="x_scale_table", align_bytes=64)
         w_scale = keep.tile([P, 4, PASSES, N], U8, name="w_scale", align_bytes=64)
-        w_stage = keep.tile([16, 4, PASSES, N], U8, name="w_stage", tag="stage_then_dec", align_bytes=64)
+        w_stage = keep.tile([16, 4, PASSES, N], U8, name="w_stage", align_bytes=64)
         nc.gpsimd.memset(x_scale_table[:].bitcast(I32), 0)
         nc.vector.memset(w_scale[:].bitcast(I32), 0)
 
-        x_table = [keep.tile([P, T], I32, name="x_table%d" % o, align_bytes=64) for o in range(PASSES)]
-        w_code = [keep.tile([P, PASSES, N], I32, name="w_code%d" % i, align_bytes=64) for i in range(4)]
-        e_raw = [keep.tile([P, PACK, w], F32, name="e_raw%d" % i, align_bytes=64) for i, (o, c, w, s) in enumerate(PIECES)]
+        KB = 1024
+        x_at = [4 * KB, 16 * KB]
+        x_table = [shared.tile([P, T], I32, name="x_table%d" % o, align_bytes=64, offset=x_at[o]) for o in range(PASSES)]
+        w_code = [None] * 4
+        e_raw = [None] * len(PIECES)
+        w_code[1] = keep.tile([P, PASSES, N], I32, name="w_code1", align_bytes=64)
+        e_raw[0] = keep.tile([P, PACK, 256], F32, name="e_raw0", align_bytes=64)
 
         def load_x(o):
             nc.sync.dma_start(out=x_table[o][:], in_=x_words[o].rearrange("p c r -> p (c r)").bitcast(I32))
@@ -62,24 +67,30 @@ def tile_picked_zcft_add_p_kernel(
             nc.scalar.dma_start(out=w_stage[:, i].bitcast(I32), in_=w_scales[i].rearrange("o r c -> r o c").bitcast(I32))
         load_x(1)
         for q in range(4):
-            nc.gpsimd.dma_start(out=x_scale_table[32 * q:32 * q + 8, :].bitcast(I32), in_=x_scales[:, 4 * q:4 * q + 4, :].bitcast(I32))
-        warm = keep.tile([P, 2], F32, name="warm")
-        nc.vector.memset(warm[:, 0:1], 0.0)
-        nc.scalar.copy(out=warm[:, 1:2], in_=warm[:, 0:1])
-        for i in (1, 3, 0, 2):
-            load_w(i)
-        for i in range(len(PIECES)):
-            load_e(i)
+            nc.scalar.dma_start(out=x_scale_table[32 * q:32 * q + 8, :].bitcast(I32), in_=x_scales[:, 4 * q:4 * q + 4, :].bitcast(I32))
+        load_w(1)
+        load_e(0)
         for q in range(4):
             nc.scalar.dma_start(out=w_scale[32 * q:32 * q + 4].bitcast(I32), in_=w_stage[4 * q:4 * q + 4].bitcast(I32))
-        dec_sb = keep.tile([P, S], F32, name="dec_sb", tag="stage_then_dec", align_bytes=64)
-        nc.sync.dma_start(out=dec_sb[:], in_=dec)
+        warm = keep.tile([16, 1], U32, name="warm")
+        nc.scalar.copy(out=warm[:], in_=w_stage[:, 3, 1, 0:4].bitcast(U32))
 
         x_code = [keep.tile([P, S], U32, name="x_code%d" % o, align_bytes=64) for o in range(PASSES)]
         x_scale = keep.tile([P, S], U8, name="x_scale", align_bytes=64)
         nc.vector.tensor_copy(x_code[0][:], x_table[0][:].bitcast(U32).indirect(offsets[:]))
-        nc.vector.tensor_copy(x_scale[:], x_scale_table[:].indirect(offsets[:]))
         nc.vector.tensor_copy(x_code[1][:], x_table[1][:].bitcast(U32).indirect(offsets[:]))
+        nc.vector.tensor_copy(x_scale[:], x_scale_table[:].indirect(offsets[:]))
+        e_raw[1] = shared.tile([P, PACK, 256], F32, name="e_raw1", align_bytes=64, offset=64)
+        load_e(1)
+        for n, i in enumerate((3, 0, 2)):
+            w_code[i] = shared.tile([P, PASSES, N], I32, name="w_code%d" % i, align_bytes=64, offset=x_at[0] + 64 + n * KB)
+            load_w(i)
+        e_raw[2] = shared.tile([P, PACK, 256], F32, name="e_raw2", align_bytes=64, offset=x_at[0] + 64 + 3 * KB)
+        load_e(2)
+        e_raw[3] = shared.tile([P, PACK, 256], F32, name="e_raw3", align_bytes=64, offset=x_at[1] + 64 - 4 * KB)
+        load_e(3)
+        dec_sb = shared.tile([P, S], F32, name="dec_sb", align_bytes=64, offset=x_at[1] + 64)
+        nc.sync.dma_start(out=dec_sb[:], in_=dec)
 
         acc = [[psum.tile([P, w], F32, name="acc%d_%d" % (b, h)) for h in range(2)] for b, (c, w) in enumerate(BLOCKS)]
 

@@ -7,7 +7,22 @@ P = 128
 PACK = 4
 K_PASS = P * PACK
 PASSES = K // K_PASS
-FLOPS = 2 * 4 * K * N * S
+QUADRANT = 32
+QUADRANTS = P // QUADRANT
+ROWS = 4
+WEIGHTS = 4
+HALVES = 2
+HALF = S // HALVES
+LINE = 4
+ALIGN = 64
+KB = 1024
+FLOPS = 2 * WEIGHTS * K * N * S
+
+E_WEIGHT = (0, 2)
+X_WEIGHT = (1, 3)
+
+PIECES = [(half, o) for half in range(HALVES) for o in range(PASSES)]
+SCALAR_COLUMNS = [128, 128, 128, 96]
 
 F32 = mybir.dt.float32
 BF16 = mybir.dt.bfloat16
@@ -18,9 +33,6 @@ U8 = mybir.dt.uint8
 FP8X4 = mybir.dt.float8_e4m3fn_x4
 ADD = mybir.AluOpType.add
 MULT = mybir.AluOpType.mult
-
-PIECES = [(0, 0, 256, 128), (1, 0, 256, 128), (0, 256, 256, 128), (1, 256, 256, 96)]
-BLOCKS = [(0, 256), (256, 256)]
 
 
 def tile_picked_zcft_add_p_kernel(
@@ -36,94 +48,116 @@ def tile_picked_zcft_add_p_kernel(
         psum = ctx.enter_context(tc.psum_pool(name="psum", bufs=1))
 
         offsets = keep.tile([P, S // 16], U16, name="offsets")
-        x_scale_table = keep.tile([P, T], U8, name="x_scale_table", align_bytes=64)
-        w_scale = keep.tile([P, 4, PASSES, N], U8, name="w_scale", align_bytes=64)
-        w_stage = keep.tile([16, 4, PASSES, N], U8, name="w_stage", align_bytes=64)
+        x_scale_table = keep.tile([P, T], U8, name="x_scale_table", align_bytes=ALIGN)
+        w_scale = keep.tile([P, WEIGHTS, PASSES, N], U8, name="w_scale", align_bytes=ALIGN)
+        w_stage = keep.tile([QUADRANTS * ROWS, WEIGHTS, PASSES, N], U8, name="w_stage", align_bytes=ALIGN)
         nc.gpsimd.memset(x_scale_table[:].bitcast(I32), 0)
         nc.vector.memset(w_scale[:].bitcast(I32), 0)
 
-        KB = 1024
         x_at = [4 * KB, 16 * KB]
-        x_table = [shared.tile([P, T], I32, name="x_table%d" % o, align_bytes=64, offset=x_at[o]) for o in range(PASSES)]
-        w_code = [None] * 4
+        x_table = [
+            shared.tile([P, T], I32, name="x_table%d" % o, align_bytes=ALIGN, offset=x_at[o]) for o in range(PASSES)
+        ]
+        w_code = [None] * WEIGHTS
         e_raw = [None] * len(PIECES)
-        w_code[1] = keep.tile([P, PASSES, N], I32, name="w_code1", align_bytes=64)
-        e_raw[0] = keep.tile([P, PACK, 256], F32, name="e_raw0", align_bytes=64)
+        w_code[X_WEIGHT[0]] = keep.tile([P, PASSES, N], I32, name="w_code1", align_bytes=ALIGN)
+        e_raw[0] = keep.tile([P, PACK, HALF], F32, name="e_raw0", align_bytes=ALIGN)
+
+        def columns(half):
+            return slice(half * HALF, (half + 1) * HALF)
 
         def load_x(o):
             nc.sync.dma_start(out=x_table[o][:], in_=x_words[o].rearrange("p c r -> p (c r)").bitcast(I32))
 
-        def load_w(i):
-            nc.sync.dma_start(out=w_code[i][:], in_=w_words[i].rearrange("o p c r -> p o (c r)").bitcast(I32))
+        def load_w(weight):
+            words = w_words[weight].rearrange("o p c r -> p o (c r)")
+            nc.sync.dma_start(out=w_code[weight][:], in_=words.bitcast(I32))
 
-        def load_e(i):
-            o, c, w, s = PIECES[i]
-            rows = eT[o * K_PASS:(o + 1) * K_PASS, c:c + w]
-            nc.sync.dma_start(out=e_raw[i][:], in_=rows.rearrange("(p j) w -> p j w", j=PACK))
+        def load_e(piece):
+            half, o = PIECES[piece]
+            rows = eT[o * K_PASS:(o + 1) * K_PASS, columns(half)]
+            nc.sync.dma_start(out=e_raw[piece][:], in_=rows.rearrange("(p t) c -> p t c", t=PACK))
 
         nc.sync.dma_start(offsets[:], offs)
         load_x(0)
-        for i in range(4):
-            nc.scalar.dma_start(out=w_stage[:, i].bitcast(I32), in_=w_scales[i].rearrange("o r c -> r o c").bitcast(I32))
+        for weight in range(WEIGHTS):
+            rows = w_scales[weight].rearrange("o b c -> b o c")
+            nc.scalar.dma_start(out=w_stage[:, weight].bitcast(I32), in_=rows.bitcast(I32))
         load_x(1)
-        for q in range(4):
-            nc.scalar.dma_start(out=x_scale_table[32 * q:32 * q + 8, :].bitcast(I32), in_=x_scales[:, 4 * q:4 * q + 4, :].bitcast(I32))
-        load_w(1)
+        for q in range(QUADRANTS):
+            nc.scalar.dma_start(
+                out=x_scale_table[QUADRANT * q:QUADRANT * q + PASSES * ROWS, :].bitcast(I32),
+                in_=x_scales[:, ROWS * q:ROWS * (q + 1), :].bitcast(I32),
+            )
+        load_w(X_WEIGHT[0])
         load_e(0)
-        for q in range(4):
-            nc.scalar.dma_start(out=w_scale[32 * q:32 * q + 4].bitcast(I32), in_=w_stage[4 * q:4 * q + 4].bitcast(I32))
-        warm = keep.tile([16, 1], U32, name="warm")
-        nc.scalar.copy(out=warm[:], in_=w_stage[:, 3, 1, 0:4].bitcast(U32))
+        for q in range(QUADRANTS):
+            nc.scalar.dma_start(
+                out=w_scale[QUADRANT * q:QUADRANT * q + ROWS].bitcast(I32),
+                in_=w_stage[ROWS * q:ROWS * (q + 1)].bitcast(I32),
+            )
 
-        x_code = [keep.tile([P, S], U32, name="x_code%d" % o, align_bytes=64) for o in range(PASSES)]
-        x_scale = keep.tile([P, S], U8, name="x_scale", align_bytes=64)
-        nc.vector.tensor_copy(x_code[0][:], x_table[0][:].bitcast(U32).indirect(offsets[:]))
-        nc.vector.tensor_copy(x_code[1][:], x_table[1][:].bitcast(U32).indirect(offsets[:]))
+        x_code = [keep.tile([P, S], U32, name="x_code%d" % o, align_bytes=ALIGN) for o in range(PASSES)]
+        x_scale = keep.tile([P, S], U8, name="x_scale", align_bytes=ALIGN)
+        for o in range(PASSES):
+            nc.vector.tensor_copy(x_code[o][:], x_table[o][:].bitcast(U32).indirect(offsets[:]))
         nc.vector.tensor_copy(x_scale[:], x_scale_table[:].indirect(offsets[:]))
-        e_raw[1] = shared.tile([P, PACK, 256], F32, name="e_raw1", align_bytes=64, offset=64)
+
+        e_raw[1] = shared.tile([P, PACK, HALF], F32, name="e_raw1", align_bytes=ALIGN, offset=x_at[0] + ALIGN - 4 * KB)
         load_e(1)
-        for n, i in enumerate((3, 0, 2)):
-            w_code[i] = shared.tile([P, PASSES, N], I32, name="w_code%d" % i, align_bytes=64, offset=x_at[0] + 64 + n * KB)
-            load_w(i)
-        e_raw[2] = shared.tile([P, PACK, 256], F32, name="e_raw2", align_bytes=64, offset=x_at[0] + 64 + 3 * KB)
+        for place, weight in enumerate((X_WEIGHT[1],) + E_WEIGHT):
+            w_code[weight] = shared.tile(
+                [P, PASSES, N], I32, name="w_code%d" % weight, align_bytes=ALIGN, offset=x_at[0] + ALIGN + place * KB
+            )
+            load_w(weight)
+        e_raw[2] = shared.tile([P, PACK, HALF], F32, name="e_raw2", align_bytes=ALIGN, offset=x_at[0] + ALIGN + 3 * KB)
         load_e(2)
-        e_raw[3] = shared.tile([P, PACK, 256], F32, name="e_raw3", align_bytes=64, offset=x_at[1] + 64 - 4 * KB)
+        e_raw[3] = shared.tile([P, PACK, HALF], F32, name="e_raw3", align_bytes=ALIGN, offset=x_at[1] + ALIGN - 4 * KB)
         load_e(3)
-        dec_sb = shared.tile([P, S], F32, name="dec_sb", align_bytes=64, offset=x_at[1] + 64)
+        dec_sb = shared.tile([P, S], F32, name="dec_sb", align_bytes=ALIGN, offset=x_at[1] + ALIGN)
         nc.sync.dma_start(out=dec_sb[:], in_=dec)
 
-        acc = [[psum.tile([P, w], F32, name="acc%d_%d" % (b, h)) for h in range(2)] for b, (c, w) in enumerate(BLOCKS)]
+        acc = [
+            [psum.tile([P, HALF], F32, name="acc%d_%d" % (half, result)) for result in range(2)]
+            for half in range(HALVES)
+        ]
 
-        def product(b, h, i, o, codes, scales, start, stop):
+        def product(half, result, weight, o, codes, scales, start, stop):
             nc.tensor.matmul_mx(
-                out=acc[b][h][:], lhsT=w_code[i][:, o, :].bitcast(FP8X4), lhsT_scale=w_scale[:, i, o, :],
-                rhs=codes.bitcast(FP8X4), rhs_scale=scales, start=start, stop=stop)
+                out=acc[half][result][:],
+                lhsT=w_code[weight][:, o, :].bitcast(FP8X4),
+                lhsT_scale=w_scale[:, weight, o, :],
+                rhs=codes.bitcast(FP8X4),
+                rhs_scale=scales,
+                start=start,
+                stop=stop,
+            )
 
         for o in range(PASSES):
-            for b, (c, w) in enumerate(BLOCKS):
-                for h in range(2):
-                    product(b, h, 2 * h + 1, o, x_code[o][:, c:c + w], x_scale[4 * o:, c:c + w], o == 0, False)
+            for half in range(HALVES):
+                for result in range(2):
+                    codes, scales = x_code[o][:, columns(half)], x_scale[ROWS * o:, columns(half)]
+                    product(half, result, X_WEIGHT[result], o, codes, scales, o == 0, False)
 
         def interleave(copy, dst, src):
-            copy(out=dst.rearrange("p (c i) t -> p c t i", i=4), in_=src.rearrange("p t (c i) -> p c t i", i=4))
+            copy(out=dst.rearrange("p (c i) t -> p c t i", i=LINE), in_=src.rearrange("p t (c i) -> p c t i", i=LINE))
 
-        for i, (o, c, w, s) in enumerate(PIECES):
-            grouped = keep.tile([P, w, PACK], BF16, name="grouped%d" % i, align_bytes=64)
-            if s > 0:
-                interleave(nc.scalar.copy, grouped[:, :s, :], e_raw[i][:, :, :s])
-            if s < w:
-                interleave(nc.vector.tensor_copy, grouped[:, s:, :], e_raw[i][:, :, s:])
-            e_code = keep.tile([P, w], U32, name="e_code%d" % i, align_bytes=64)
-            e_scale = keep.tile([P, w], U8, name="e_scale%d" % i, align_bytes=64)
-            nc.vector.quantize_mx(out=e_code[:].bitcast(FP8X4), scales=e_scale[:], in_=grouped[:].rearrange("p w j -> p (w j)"))
-            for b, (bc, bw) in enumerate(BLOCKS):
-                if c <= bc < c + w:
-                    cols = slice(bc - c, bc - c + bw)
-                    for h in range(2):
-                        product(b, h, 2 * h, o, e_code[:, cols], e_scale[:, cols], False, o == PASSES - 1)
-                    if o == PASSES - 1:
-                        scaled = keep.tile([P, bw], F32, name="scaled%d" % b, align_bytes=64)
-                        result = keep.tile([P, bw], F32, name="result%d" % b, align_bytes=64)
-                        nc.vector.scalar_tensor_tensor(scaled[:], acc[b][0][:], 1.0, dec_sb[:, bc:bc + bw], ADD, MULT)
-                        nc.vector.tensor_tensor(result[:], acc[b][1][:], scaled[:], ADD)
-                        nc.sync.dma_start(out=out[:, bc:bc + bw], in_=result[:])
+        for piece, (half, o) in enumerate(PIECES):
+            grouped = keep.tile([P, HALF, PACK], BF16, name="grouped%d" % piece, align_bytes=ALIGN)
+            split = SCALAR_COLUMNS[piece]
+            interleave(nc.scalar.copy, grouped[:, :split, :], e_raw[piece][:, :, :split])
+            interleave(nc.vector.tensor_copy, grouped[:, split:, :], e_raw[piece][:, :, split:])
+            e_code = keep.tile([P, HALF], U32, name="e_code%d" % piece, align_bytes=ALIGN)
+            e_scale = keep.tile([P, HALF], U8, name="e_scale%d" % piece, align_bytes=ALIGN)
+            nc.vector.quantize_mx(
+                out=e_code[:].bitcast(FP8X4), scales=e_scale[:], in_=grouped[:].rearrange("p c t -> p (c t)")
+            )
+            last = o == PASSES - 1
+            for result in range(2):
+                product(half, result, E_WEIGHT[result], o, e_code[:], e_scale[:], False, last)
+            if last:
+                scaled = keep.tile([P, HALF], F32, name="scaled%d" % half, align_bytes=ALIGN)
+                combined = keep.tile([P, HALF], F32, name="result%d" % half, align_bytes=ALIGN)
+                nc.vector.scalar_tensor_tensor(scaled[:], acc[half][0][:], 1.0, dec_sb[:, columns(half)], ADD, MULT)
+                nc.vector.tensor_tensor(combined[:], acc[half][1][:], scaled[:], ADD)
+                nc.sync.dma_start(out=out[:, columns(half)], in_=combined[:])

from contextlib import ExitStack

import concourse.mybir as mybir

K, T, S, N = 1024, 1024, 512, 128
P = 128
PACK = 4
K_PASS = P * PACK
PASSES = K // K_PASS
QUADRANT = 32
QUADRANTS = P // QUADRANT
ROWS = 4
WEIGHTS = 4
HALVES = 2
HALF = S // HALVES
LINE = 4
ALIGN = 64
KB = 1024
FLOPS = 2 * WEIGHTS * K * N * S

E_WEIGHT = (0, 2)
X_WEIGHT = (1, 3)

PIECES = [(half, o) for half in range(HALVES) for o in range(PASSES)]
SCALAR_COLUMNS = [128, 128, 128, 96]

F32 = mybir.dt.float32
BF16 = mybir.dt.bfloat16
I32 = mybir.dt.int32
U32 = mybir.dt.uint32
U16 = mybir.dt.uint16
U8 = mybir.dt.uint8
FP8X4 = mybir.dt.float8_e4m3fn_x4
ADD = mybir.AluOpType.add
MULT = mybir.AluOpType.mult


def tile_picked_zcft_add_p_kernel(
    tc, x_words, x_scales, eT, w1_words, w1_scales, w2_words, w2_scales,
    w3_words, w3_scales, w4_words, w4_scales, dec, offs, out
):
    nc = tc.nc
    w_words = [w1_words, w2_words, w3_words, w4_words]
    w_scales = [w1_scales, w2_scales, w3_scales, w4_scales]
    with ExitStack() as ctx:
        keep = ctx.enter_context(tc.tile_pool(name="keep", bufs=1))
        shared = ctx.enter_context(tc.tile_pool(name="shared", bufs=1))
        psum = ctx.enter_context(tc.psum_pool(name="psum", bufs=1))

        offsets = keep.tile([P, S // 16], U16, name="offsets")
        x_scale_table = keep.tile([P, T], U8, name="x_scale_table", align_bytes=ALIGN)
        w_scale = keep.tile([P, WEIGHTS, PASSES, N], U8, name="w_scale", align_bytes=ALIGN)
        w_stage = keep.tile([QUADRANTS * ROWS, WEIGHTS, PASSES, N], U8, name="w_stage", align_bytes=ALIGN)
        nc.gpsimd.memset(x_scale_table[:].bitcast(I32), 0)
        nc.vector.memset(w_scale[:].bitcast(I32), 0)

        x_at = [4 * KB, 16 * KB]
        x_table = [
            shared.tile([P, T], I32, name="x_table%d" % o, align_bytes=ALIGN, offset=x_at[o]) for o in range(PASSES)
        ]
        w_code = [None] * WEIGHTS
        e_raw = [None] * len(PIECES)
        w_code[X_WEIGHT[0]] = keep.tile([P, PASSES, N], I32, name="w_code1", align_bytes=ALIGN)
        e_raw[0] = keep.tile([P, PACK, HALF], F32, name="e_raw0", align_bytes=ALIGN)

        def columns(half):
            return slice(half * HALF, (half + 1) * HALF)

        def load_x(o):
            nc.sync.dma_start(out=x_table[o][:], in_=x_words[o].rearrange("p c r -> p (c r)").bitcast(I32))

        def load_w(weight):
            words = w_words[weight].rearrange("o p c r -> p o (c r)")
            nc.sync.dma_start(out=w_code[weight][:], in_=words.bitcast(I32))

        def load_e(piece):
            half, o = PIECES[piece]
            rows = eT[o * K_PASS:(o + 1) * K_PASS, columns(half)]
            nc.sync.dma_start(out=e_raw[piece][:], in_=rows.rearrange("(p t) c -> p t c", t=PACK))

        nc.sync.dma_start(offsets[:], offs)
        load_x(0)
        for weight in range(WEIGHTS):
            rows = w_scales[weight].rearrange("o b c -> b o c")
            nc.scalar.dma_start(out=w_stage[:, weight].bitcast(I32), in_=rows.bitcast(I32))
        load_x(1)
        for q in range(QUADRANTS):
            nc.scalar.dma_start(
                out=x_scale_table[QUADRANT * q:QUADRANT * q + PASSES * ROWS, :].bitcast(I32),
                in_=x_scales[:, ROWS * q:ROWS * (q + 1), :].bitcast(I32),
            )
        load_w(X_WEIGHT[0])
        load_e(0)
        for q in range(QUADRANTS):
            nc.scalar.dma_start(
                out=w_scale[QUADRANT * q:QUADRANT * q + ROWS].bitcast(I32),
                in_=w_stage[ROWS * q:ROWS * (q + 1)].bitcast(I32),
            )

        x_code = [keep.tile([P, S], U32, name="x_code%d" % o, align_bytes=ALIGN) for o in range(PASSES)]
        x_scale = keep.tile([P, S], U8, name="x_scale", align_bytes=ALIGN)
        for o in range(PASSES):
            nc.vector.tensor_copy(x_code[o][:], x_table[o][:].bitcast(U32).indirect(offsets[:]))
        nc.vector.tensor_copy(x_scale[:], x_scale_table[:].indirect(offsets[:]))

        e_raw[1] = shared.tile([P, PACK, HALF], F32, name="e_raw1", align_bytes=ALIGN, offset=x_at[0] + ALIGN - 4 * KB)
        load_e(1)
        for place, weight in enumerate((X_WEIGHT[1],) + E_WEIGHT):
            w_code[weight] = shared.tile(
                [P, PASSES, N], I32, name="w_code%d" % weight, align_bytes=ALIGN, offset=x_at[0] + ALIGN + place * KB
            )
            load_w(weight)
        e_raw[2] = shared.tile([P, PACK, HALF], F32, name="e_raw2", align_bytes=ALIGN, offset=x_at[0] + ALIGN + 3 * KB)
        load_e(2)
        e_raw[3] = shared.tile([P, PACK, HALF], F32, name="e_raw3", align_bytes=ALIGN, offset=x_at[1] + ALIGN - 4 * KB)
        load_e(3)
        dec_sb = shared.tile([P, S], F32, name="dec_sb", align_bytes=ALIGN, offset=x_at[1] + ALIGN)
        nc.sync.dma_start(out=dec_sb[:], in_=dec)

        acc = [
            [psum.tile([P, HALF], F32, name="acc%d_%d" % (half, result)) for result in range(2)]
            for half in range(HALVES)
        ]

        def product(half, result, weight, o, codes, scales, start, stop):
            nc.tensor.matmul_mx(
                out=acc[half][result][:],
                lhsT=w_code[weight][:, o, :].bitcast(FP8X4),
                lhsT_scale=w_scale[:, weight, o, :],
                rhs=codes.bitcast(FP8X4),
                rhs_scale=scales,
                start=start,
                stop=stop,
            )

        for o in range(PASSES):
            for half in range(HALVES):
                for result in range(2):
                    codes, scales = x_code[o][:, columns(half)], x_scale[ROWS * o:, columns(half)]
                    product(half, result, X_WEIGHT[result], o, codes, scales, o == 0, False)

        def interleave(copy, dst, src):
            copy(out=dst.rearrange("p (c i) t -> p c t i", i=LINE), in_=src.rearrange("p t (c i) -> p c t i", i=LINE))

        for piece, (half, o) in enumerate(PIECES):
            grouped = keep.tile([P, HALF, PACK], BF16, name="grouped%d" % piece, align_bytes=ALIGN)
            split = SCALAR_COLUMNS[piece]
            interleave(nc.scalar.copy, grouped[:, :split, :], e_raw[piece][:, :, :split])
            interleave(nc.vector.tensor_copy, grouped[:, split:, :], e_raw[piece][:, :, split:])
            e_code = keep.tile([P, HALF], U32, name="e_code%d" % piece, align_bytes=ALIGN)
            e_scale = keep.tile([P, HALF], U8, name="e_scale%d" % piece, align_bytes=ALIGN)
            nc.vector.quantize_mx(
                out=e_code[:].bitcast(FP8X4), scales=e_scale[:], in_=grouped[:].rearrange("p c t -> p (c t)")
            )
            last = o == PASSES - 1
            for result in range(2):
                product(half, result, E_WEIGHT[result], o, e_code[:], e_scale[:], False, last)
            if last:
                scaled = keep.tile([P, HALF], F32, name="scaled%d" % half, align_bytes=ALIGN)
                combined = keep.tile([P, HALF], F32, name="result%d" % half, align_bytes=ALIGN)
                nc.vector.scalar_tensor_tensor(scaled[:], acc[half][0][:], 1.0, dec_sb[:, columns(half)], ADD, MULT)
                nc.vector.tensor_tensor(combined[:], acc[half][1][:], scaled[:], ADD)
                nc.sync.dma_start(out=out[:, columns(half)], in_=combined[:])
